import numpy as np
import ml_dtypes


def mxq(x, axis, fmt="e4m3"):
    dtype, down = {"e4m3": (ml_dtypes.float8_e4m3fn, 7), "e5m2": (ml_dtypes.float8_e5m2, 14)}[fmt]
    v = np.moveaxis(np.asarray(x, np.float32).astype(ml_dtypes.bfloat16).astype(np.float64), axis, -1)
    blocks = v.reshape(v.shape[:-1] + (-1, 32))
    amax = np.abs(blocks).max(-1, keepdims=True)
    byte = np.maximum(np.where(amax > 0, np.frexp(amax)[1] - 1 + 127, 0) - down, 1)
    scale = np.exp2(byte - 127.0)
    codes = (blocks / scale).astype(np.float32).astype(dtype).astype(np.float64)
    return np.moveaxis((codes * scale).reshape(v.shape), -1, axis)


WIDE = False


def mx_kscale(k):
    if not WIDE:
        return np.ones(k)
    levels = np.array([30, -30])
    if k % 512:
        return np.exp2(np.random.permutation(np.resize(levels, k // 32))).repeat(32)
    a = np.empty((k // 512, 16))
    for p in range(k // 512):
        a[p, :8] = np.random.permutation(np.resize(levels, 8))
        for g in range(8):
            far = levels[np.abs(levels - a[p, g]) >= 10]
            a[p, g + 8] = far[np.random.randint(len(far))]
    return np.exp2(a.ravel()).repeat(32)


BF16 = ml_dtypes.bfloat16


def bf(x):
    return np.asarray(x, np.float32).astype(BF16)


def f64(x):
    return np.asarray(x).astype(np.float64)


E2M1 = np.array([0.0, 0.5, 1.0, 1.5, 2.0, 3.0, 4.0, 6.0, -0.0, -0.5, -1.0, -1.5, -2.0, -3.0, -4.0, -6.0])


def pack_weight(w, fmt):
    k, n = w.shape
    w = f64(bf(w)).reshape(k // 32, 32, n)
    amax = np.abs(w).max(1)
    if fmt in ("e4m3", "e5m2"):
        byte = np.frexp(amax)[1] - 1 + 127 - (7 if fmt == "e4m3" else 14)
    else:
        mant, ex = np.frexp(amax / 6.0)
        byte = np.where(mant > 0.5, ex, ex - 1) + 127
    byte = np.clip(np.where(amax > 0, byte, 1), 1, 254)
    scaled = (w * np.exp2(127.0 - byte)[:, None, :]).reshape(k, n).astype(np.float32)
    by_word = np.ascontiguousarray(scaled.reshape(k // 512, 128, 4, n).transpose(0, 1, 3, 2))
    if fmt in ("e4m3", "e5m2"):
        words = by_word.astype(ml_dtypes.float8_e4m3fn if fmt == "e4m3" else ml_dtypes.float8_e5m2).view(np.uint8)
    else:
        c = by_word.astype(ml_dtypes.float4_e2m1fn).view(np.uint8) & 0xF
        words = c[..., 0::2] | (c[..., 1::2] << 4)
    return np.ascontiguousarray(words), np.ascontiguousarray(byte.astype(np.uint8).reshape(k // 512, 16, n))


def unpack_weight(words, scales, fmt):
    g, p, n, _ = words.shape
    if fmt in ("e4m3", "e5m2"):
        vals = np.ascontiguousarray(words).view(ml_dtypes.float8_e4m3fn if fmt == "e4m3" else ml_dtypes.float8_e5m2).astype(np.float64)
    else:
        nib = np.empty((g, p, n, 4), np.uint8)
        nib[..., 0::2] = words & 0xF
        nib[..., 1::2] = words >> 4
        vals = E2M1[nib]
    vals = vals * np.repeat(np.exp2(scales.astype(np.float64) - 127.0), 8, axis=1)[..., None]
    return vals.transpose(0, 1, 3, 2).reshape(g * 512, n)


T, F, R, D = 1024, 4096, 512, 2048


def setup_inputs():
    s, r = mx_kscale(F), mx_kscale(R)
    G = np.random.standard_normal((F, T)) * np.exp(0.5 * np.random.standard_normal((F, T))) * s[:, None]
    G_words, G_scales = pack_weight(G, "e5m2")
    return {"dkv_words": G_words,
            "dkv_scales": G_scales,
            "w_up": bf(np.random.standard_normal((R, F)) / np.sqrt(F) / s),
            "dc_later": bf(0.5 * np.random.standard_normal((T, R))),
            "gate": bf((1 + 0.5 * np.random.standard_normal((T, R))) * r),
            "w_down": bf(np.random.standard_normal((D, R)) / np.sqrt(R) / r),
            "dh_skip": bf(np.random.standard_normal((T, D)))}


def reference(dkv_words, dkv_scales, w_up, dc_later, gate, w_down, dh_skip):
    g = unpack_weight(dkv_words, dkv_scales, "e5m2")
    wu = mxq(f64(w_up), 1, "e4m3")
    dc = (g.T @ wu.T) + f64(dc_later)
    z = dc * f64(gate)
    wd = mxq(f64(w_down), 1, "e4m3")
    dh = (mxq(z, 1, "e5m2") @ wd.T) + f64(dh_skip)
    return dc, dh

@@ -1,0 +1,290 @@
+from contextlib import ExitStack
+
+import concourse.mybir as mybir
+from concourse.masks import make_identity
+
+T, F, R, D = 1024, 4096, 512, 2048
+FLOPS = 2 * T * F * R + 2 * T * R * D
+
+F32 = mybir.dt.float32
+BF16 = mybir.dt.bfloat16
+U32 = mybir.dt.uint32
+I32 = mybir.dt.int32
+U8 = mybir.dt.uint8
+E4M3 = mybir.dt.float8_e4m3fn_x4
+E5M2 = mybir.dt.float8_e5m2_x4
+ADD = mybir.AluOpType.add
+MULT = mybir.AluOpType.mult
+
+P = 128
+PASSES = F // 512
+RT = R // P
+TT = T // P
+HALF = TT // 2
+DB = D // 512
+
+
+def tile_latent_cache_backward_e3_kernel(
+    tc, dkv_words, dkv_scales, w_up, dc_later, gate, w_down, dh_skip, out_dc, out_dh
+):
+    nc = tc.nc
+    with ExitStack() as ctx:
+        keep = ctx.enter_context(tc.tile_pool(name="keep", bufs=1))
+        stage = ctx.enter_context(tc.tile_pool(name="stage", bufs=8))
+        group = ctx.enter_context(tc.tile_pool(name="group", bufs=4))
+        small = ctx.enter_context(tc.tile_pool(name="small", bufs=4))
+        accs = ctx.enter_context(tc.psum_pool(name="accs", bufs=4))
+        work = ctx.enter_context(tc.psum_pool(name="work", bufs=4))
+
+        ident = keep.tile([P, P], F32, name="ident")
+        make_identity(nc, ident[:])
+
+        g_words = keep.tile([P, PASSES, T], U32, name="g_words", align_bytes=64)
+        g_scales = keep.tile([P, PASSES, T], U8, name="g_scales", align_bytes=64)
+        up_codes = keep.tile([P, PASSES, R], U32, name="up_codes", align_bytes=64)
+        up_scales = keep.tile([P, PASSES, R], U8, name="up_scales", align_bytes=64)
+        down_codes = keep.tile([P, D], U32, name="down_codes", align_bytes=64)
+        down_scales = keep.tile([P, D], U8, name="down_scales", align_bytes=64)
+        skip = keep.tile([P, TT, D], BF16, name="skip", align_bytes=64)
+        later = keep.tile([P, TT, R], BF16, name="later", align_bytes=64)
+        gates = keep.tile([P, TT, R], BF16, name="gates", align_bytes=64)
+
+        with tc.manual_schedule():
+            nc.vector.memset(g_scales[:].rearrange("p g n -> p (g n)").bitcast(I32), 0)
+            up_raw = []
+            for rt in range(RT):
+                raw = stage.tile([P, F], BF16, name="up_raw", tag="stage", align_bytes=64)
+                nc.sync.dma_start(out=raw[:], in_=w_up[rt * P : (rt + 1) * P, :])
+                up_raw.append(raw)
+            for q in range(4):
+                nc.sync.dma_start(
+                    out=g_scales[32 * q : 32 * q + 4, :, :].bitcast(I32),
+                    in_=dkv_scales[:, 4 * q : 4 * q + 4, :].rearrange("g q n -> q g n").bitcast(I32),
+                )
+
+            def load_g(g, h):
+                cols = slice(h * (T // 2), (h + 1) * (T // 2))
+                nc.sync.dma_start(
+                    out=g_words[:, g : g + 4, cols].bitcast(I32),
+                    in_=dkv_words[g : g + 4, :, cols, :].rearrange("g p n t -> p g (n t)").bitcast(I32),
+                )
+
+            def load_half(tile, src, h):
+                nc.sync.dma_start(
+                    out=tile[:, h * HALF : (h + 1) * HALF, :],
+                    in_=src[h * (T // 2) : (h + 1) * (T // 2), :].rearrange("(i p) r -> p i r", p=P),
+                )
+
+            load_g(0, 0)
+            load_g(4, 0)
+            load_half(later, dc_later, 0)
+            load_half(gates, gate, 0)
+            down_raw = []
+            for h in range(2):
+                raw = stage.tile([P, 2, 4, R], BF16, name="down_raw", tag="stage", align_bytes=64)
+                nc.sync.dma_start(
+                    out=raw[:].rearrange("p b a r -> p b (a r)"),
+                    in_=w_down[h * 1024 : (h + 1) * 1024, :].rearrange("(b p a) r -> p b (a r)", p=P, a=4),
+                )
+                down_raw.append(raw)
+            for i in range(TT):
+                if i == 2:
+                    load_g(0, 1)
+                    load_g(4, 1)
+                    load_half(later, dc_later, 1)
+                    load_half(gates, gate, 1)
+                nc.sync.dma_start(out=skip[:, i, :], in_=dh_skip[i * P : (i + 1) * P, :])
+
+            pairs = []
+            for j in range(PASSES // 2):
+                pairs.append(group.tile([P, 2, R, 4], BF16, name="grouped", tag="grouped", align_bytes=64))
+            for rt in range(RT):
+                words = up_raw[rt][:].bitcast(F32)
+                for j in range(PASSES // 2):
+                    bank = work.tile([P, 2, 2, P], F32, name="bank", tag="bank")
+                    for gg in range(2):
+                        for u in range(2):
+                            first = 256 * (2 * j + gg)
+                            nc.tensor.transpose(
+                                bank[:, gg, u, :], words[:, first + u : first + 256 : 2], ident[:]
+                            )
+                    dst = pairs[j][:].rearrange("p g r j -> p (g r j)").bitcast(F32)
+                    dst = dst.rearrange("p (g r u) -> p g r u", g=2, u=2)
+                    nc.scalar.copy(
+                        out=dst[:, :, rt * P : (rt + 1) * P, :], in_=bank[:].rearrange("p g u r -> p g r u")
+                    )
+                    if rt == RT - 1:
+                        for gg in range(2):
+                            g = 2 * j + gg
+                            nc.vector.quantize_mx(
+                                out=up_codes[:, g, :].bitcast(E4M3),
+                                scales=up_scales[:, g, :],
+                                in_=pairs[j][:, gg, :, :].rearrange("p r j -> p (r j)"),
+                            )
+
+            acc = {}
+            z_tiles = {}
+            z_codes = {}
+            dc_half = {}
+
+            def stage1_pass(i, g):
+                cols = slice(i * P, (i + 1) * P)
+                nc.tensor.matmul_mx(
+                    out=acc[i][:],
+                    lhsT=g_words[:, g, cols].bitcast(E5M2),
+                    lhsT_scale=g_scales[:, g, cols],
+                    rhs=up_codes[:, g, :].bitcast(E4M3),
+                    rhs_scale=up_scales[:, g, :],
+                    start=(g == 0),
+                    stop=(g == PASSES - 1),
+                )
+
+            def open_acc(i):
+                acc[i] = accs.tile([P, R], F32, name="acc", tag="acc")
+
+            def stage1(i):
+                open_acc(i)
+                for g in range(PASSES):
+                    stage1_pass(i, g)
+
+            def add_later(i):
+                h = i // HALF
+                if i % HALF == 0:
+                    dc_half[h] = stage.tile([P, HALF, R], F32, name="dc_half", tag="stage", align_bytes=64)
+                nc.vector.tensor_tensor(
+                    out=dc_half[h][:, i % HALF, :], in0=acc[i][:], in1=later[:, i, :], op=ADD
+                )
+
+            def times_gate(i):
+                z = small.tile([P, R], BF16, name="z", tag="z", align_bytes=64)
+                nc.vector.tensor_tensor(
+                    out=z[:], in0=dc_half[i // HALF][:, i % HALF, :], in1=gates[:, i, :], op=MULT
+                )
+                z_tiles[i] = z
+
+            def store_dc(h):
+                nc.sync.dma_start(
+                    out=out_dc[h * (T // 2) : (h + 1) * (T // 2), :].rearrange("(i p) r -> p i r", p=P),
+                    in_=dc_half[h][:],
+                )
+
+            def turn_z(i0):
+                bank = work.tile([P, 2, 2, P], F32, name="bank", tag="bank")
+                for i in range(2):
+                    words = z_tiles[i0 + i][:].bitcast(F32)
+                    for u in range(2):
+                        nc.tensor.transpose(bank[:, i, u, :], words[:, u : R // 2 : 2], ident[:])
+                grouped = small.tile([P, 2, P, 4], BF16, name="z_grouped", tag="z_grouped", bufs=2, align_bytes=64)
+                dst = grouped[:].rearrange("p i t j -> p (i t j)").bitcast(F32)
+                nc.scalar.copy(
+                    out=dst.rearrange("p (i t u) -> p i t u", i=2, u=2),
+                    in_=bank[:].rearrange("p i u t -> p i t u"),
+                )
+                return grouped
+
+            def quantise_z(i0, grouped):
+                codes = small.tile([P, 2 * P], U32, name="z_code", tag="z_code", align_bytes=64)
+                scales = small.tile([P, 2 * P], U8, name="z_scale", tag="z_scale", align_bytes=64)
+                nc.vector.quantize_mx(
+                    out=codes[:].bitcast(E5M2),
+                    scales=scales[:],
+                    in_=grouped[:].rearrange("p i t j -> p (i t j)"),
+                )
+                for i in range(2):
+                    cols = slice(i * P, (i + 1) * P)
+                    z_codes[i0 + i] = (codes[:, cols], scales[:, cols])
+
+            def turn_down(b):
+                words = down_raw[b // 2][:].rearrange("p b a r -> p (b a r)").bitcast(F32)
+                grouped = group.tile([P, 512, 4], BF16, name="grouped", tag="grouped", align_bytes=64)
+                dst = grouped[:].rearrange("p d j -> p (d j)").bitcast(F32)
+                dst = dst.rearrange("p (q a u) -> p q a u", a=4, u=2)
+                for half in range(2):
+                    bank = work.tile([P, 2, 2, P], F32, name="bank", tag="bank")
+                    for aa in range(2):
+                        first = (b % 2) * 1024 + (2 * half + aa) * 256
+                        for u in range(2):
+                            nc.tensor.transpose(
+                                bank[:, aa, u, :], words[:, first + u : first + 256 : 2], ident[:]
+                            )
+                    nc.scalar.copy(
+                        out=dst[:, :, 2 * half : 2 * half + 2, :], in_=bank[:].rearrange("p a u q -> p q a u")
+                    )
+                return grouped
+
+            def quantise_down(b, grouped):
+                cols = slice(b * 512, (b + 1) * 512)
+                nc.vector.quantize_mx(
+                    out=down_codes[:, cols].bitcast(E4M3),
+                    scales=down_scales[:, cols],
+                    in_=grouped[:].rearrange("p d j -> p (d j)"),
+                )
+
+            def stage2(i):
+                codes, scales = z_codes[i]
+                banks = []
+                for b in range(DB):
+                    cols = slice(b * 512, (b + 1) * 512)
+                    bank = work.tile([P, 512], F32, name="bank", tag="bank")
+                    nc.tensor.matmul_mx(
+                        out=bank[:],
+                        lhsT=codes.bitcast(E5M2),
+                        lhsT_scale=scales,
+                        rhs=down_codes[:, cols].bitcast(E4M3),
+                        rhs_scale=down_scales[:, cols],
+                        start=True,
+                        stop=True,
+                    )
+                    banks.append(bank)
+                return banks
+
+            def finish(i, banks):
+                dh = stage.tile([P, D], F32, name="dh", tag="stage", align_bytes=64)
+                for b in range(DB):
+                    cols = slice(b * 512, (b + 1) * 512)
+                    nc.vector.tensor_tensor(out=dh[:, cols], in0=banks[b][:], in1=skip[:, i, cols], op=ADD)
+                nc.sync.dma_start(out=out_dh[i * P : (i + 1) * P, :], in_=dh[:])
+
+            def dc_pair(i):
+                add_later(i)
+                add_later(i + 1)
+                times_gate(i)
+                times_gate(i + 1)
+
+            open_acc(0)
+            open_acc(1)
+            for g in range(PASSES):
+                for i in range(2):
+                    stage1_pass(i, g)
+            dc_pair(0)
+            d0 = turn_down(0)
+            d1 = turn_down(1)
+            quantise_down(0, d0)
+            quantise_down(1, d1)
+            turned = turn_z(0)
+            quantise_z(0, turned)
+            d2 = turn_down(2)
+            d3 = turn_down(3)
+            quantise_down(2, d2)
+            quantise_down(3, d3)
+
+            for i in range(0, TT, 2):
+                banks = stage2(i)
+                if i + 2 < TT:
+                    stage1(i + 2)
+                finish(i, banks)
+                if i + 2 < TT:
+                    add_later(i + 2)
+                banks = stage2(i + 1)
+                if i + 2 < TT:
+                    stage1(i + 3)
+                    finish(i + 1, banks)
+                    add_later(i + 3)
+                    times_gate(i + 2)
+                    times_gate(i + 3)
+                    if (i + 4) % HALF == 0:
+                        store_dc((i + 2) // HALF)
+                    turned = turn_z(i + 2)
+                    quantise_z(i + 2, turned)
+                else:
+                    finish(i + 1, banks)

@@ -51,16 +51,24 @@ def tile_latent_cache_backward_e3_kernel(
 
         with tc.manual_schedule():
             nc.vector.memset(g_scales[:].rearrange("p g n -> p (g n)").bitcast(I32), 0)
+            for q in range(4):
+                nc.gpsimd.dma_start(
+                    out=g_scales[32 * q : 32 * q + 4, :, :].bitcast(I32),
+                    in_=dkv_scales[:, 4 * q : 4 * q + 4, :].rearrange("g q n -> q g n").bitcast(I32),
+                )
+            down_raw = []
+            for h in range(2):
+                raw = stage.tile([P, 2, 4, R], BF16, name="down_raw", tag="stage", align_bytes=64)
+                nc.sync.dma_start(
+                    out=raw[:].rearrange("p b a r -> p b (a r)"),
+                    in_=w_down[h * 1024 : (h + 1) * 1024, :].rearrange("(b p a) r -> p b (a r)", p=P, a=4),
+                )
+                down_raw.append(raw)
             up_raw = []
             for rt in range(RT):
                 raw = stage.tile([P, F], BF16, name="up_raw", tag="stage", align_bytes=64)
                 nc.sync.dma_start(out=raw[:], in_=w_up[rt * P : (rt + 1) * P, :])
                 up_raw.append(raw)
-            for q in range(4):
-                nc.sync.dma_start(
-                    out=g_scales[32 * q : 32 * q + 4, :, :].bitcast(I32),
-                    in_=dkv_scales[:, 4 * q : 4 * q + 4, :].rearrange("g q n -> q g n").bitcast(I32),
-                )
 
             def load_g(g, h):
                 cols = slice(h * (T // 2), (h + 1) * (T // 2))
@@ -79,22 +87,55 @@ def tile_latent_cache_backward_e3_kernel(
             load_g(4, 0)
             load_half(later, dc_later, 0)
             load_half(gates, gate, 0)
-            down_raw = []
-            for h in range(2):
-                raw = stage.tile([P, 2, 4, R], BF16, name="down_raw", tag="stage", align_bytes=64)
-                nc.sync.dma_start(
-                    out=raw[:].rearrange("p b a r -> p b (a r)"),
-                    in_=w_down[h * 1024 : (h + 1) * 1024, :].rearrange("(b p a) r -> p b (a r)", p=P, a=4),
-                )
-                down_raw.append(raw)
             for i in range(TT):
-                if i == 2:
+                if i == 1:
                     load_g(0, 1)
                     load_g(4, 1)
                     load_half(later, dc_later, 1)
                     load_half(gates, gate, 1)
                 nc.sync.dma_start(out=skip[:, i, :], in_=dh_skip[i * P : (i + 1) * P, :])
 
+            count = [0]
+
+            def copy_out(out, in_):
+                count[0] += 1
+                if count[0] % 3 == 0:
+                    nc.vector.tensor_copy(out=out, in_=in_)
+                else:
+                    nc.scalar.copy(out=out, in_=in_)
+
+            def turn_down(b):
+                words = down_raw[b // 2][:].rearrange("p b a r -> p (b a r)").bitcast(F32)
+                grouped = group.tile([P, 512, 4], BF16, name="grouped", tag="grouped", align_bytes=64)
+                dst = grouped[:].rearrange("p d j -> p (d j)").bitcast(F32)
+                dst = dst.rearrange("p (q a u) -> p q a u", a=4, u=2)
+                for half in range(2):
+                    bank = work.tile([P, 2, 2, P], F32, name="bank", tag="bank")
+                    for aa in range(2):
+                        first = (b % 2) * 1024 + (2 * half + aa) * 256
+                        for u in range(2):
+                            nc.tensor.transpose(
+                                bank[:, aa, u, :], words[:, first + u : first + 256 : 2], ident[:]
+                            )
+                    copy_out(
+                        out=dst[:, :, 2 * half : 2 * half + 2, :], in_=bank[:].rearrange("p a u q -> p q a u")
+                    )
+                return grouped
+
+            def quantise_down(b, grouped):
+                cols = slice(b * 512, (b + 1) * 512)
+                nc.vector.quantize_mx(
+                    out=down_codes[:, cols].bitcast(E4M3),
+                    scales=down_scales[:, cols],
+                    in_=grouped[:].rearrange("p d j -> p (d j)"),
+                )
+
+            turned = [turn_down(0), turn_down(1)]
+            quantise_down(0, turned[0])
+            quantise_down(1, turned[1])
+            turned = [turn_down(2), turn_down(3)]
+            quantise_down(2, turned[0])
+            quantise_down(3, turned[1])
             pairs = []
             for j in range(PASSES // 2):
                 pairs.append(group.tile([P, 2, R, 4], BF16, name="grouped", tag="grouped", align_bytes=64))
@@ -110,7 +151,7 @@ def tile_latent_cache_backward_e3_kernel(
                             )
                     dst = pairs[j][:].rearrange("p g r j -> p (g r j)").bitcast(F32)
                     dst = dst.rearrange("p (g r u) -> p g r u", g=2, u=2)
-                    nc.scalar.copy(
+                    copy_out(
                         out=dst[:, :, rt * P : (rt + 1) * P, :], in_=bank[:].rearrange("p g u r -> p g r u")
                     )
                     if rt == RT - 1:
@@ -157,7 +198,7 @@ def tile_latent_cache_backward_e3_kernel(
 
             def times_gate(i):
                 z = small.tile([P, R], BF16, name="z", tag="z", align_bytes=64)
-                nc.vector.tensor_tensor(
+                nc.gpsimd.tensor_tensor(
                     out=z[:], in0=dc_half[i // HALF][:, i % HALF, :], in1=gates[:, i, :], op=MULT
                 )
                 z_tiles[i] = z
@@ -194,32 +235,6 @@ def tile_latent_cache_backward_e3_kernel(
                     cols = slice(i * P, (i + 1) * P)
                     z_codes[i0 + i] = (codes[:, cols], scales[:, cols])
 
-            def turn_down(b):
-                words = down_raw[b // 2][:].rearrange("p b a r -> p (b a r)").bitcast(F32)
-                grouped = group.tile([P, 512, 4], BF16, name="grouped", tag="grouped", align_bytes=64)
-                dst = grouped[:].rearrange("p d j -> p (d j)").bitcast(F32)
-                dst = dst.rearrange("p (q a u) -> p q a u", a=4, u=2)
-                for half in range(2):
-                    bank = work.tile([P, 2, 2, P], F32, name="bank", tag="bank")
-                    for aa in range(2):
-                        first = (b % 2) * 1024 + (2 * half + aa) * 256
-                        for u in range(2):
-                            nc.tensor.transpose(
-                                bank[:, aa, u, :], words[:, first + u : first + 256 : 2], ident[:]
-                            )
-                    nc.scalar.copy(
-                        out=dst[:, :, 2 * half : 2 * half + 2, :], in_=bank[:].rearrange("p a u q -> p q a u")
-                    )
-                return grouped
-
-            def quantise_down(b, grouped):
-                cols = slice(b * 512, (b + 1) * 512)
-                nc.vector.quantize_mx(
-                    out=down_codes[:, cols].bitcast(E4M3),
-                    scales=down_scales[:, cols],
-                    in_=grouped[:].rearrange("p d j -> p (d j)"),
-                )
-
             def stage2(i):
                 codes, scales = z_codes[i]
                 banks = []
@@ -245,46 +260,36 @@ def tile_latent_cache_backward_e3_kernel(
                     nc.vector.tensor_tensor(out=dh[:, cols], in0=banks[b][:], in1=skip[:, i, cols], op=ADD)
                 nc.sync.dma_start(out=out_dh[i * P : (i + 1) * P, :], in_=dh[:])
 
-            def dc_pair(i):
-                add_later(i)
-                add_later(i + 1)
-                times_gate(i)
-                times_gate(i + 1)
-
             open_acc(0)
             open_acc(1)
             for g in range(PASSES):
                 for i in range(2):
                     stage1_pass(i, g)
-            dc_pair(0)
-            d0 = turn_down(0)
-            d1 = turn_down(1)
-            quantise_down(0, d0)
-            quantise_down(1, d1)
+            for i in range(2):
+                add_later(i)
+                times_gate(i)
+            for i in range(2, 4):
+                stage1(i)
+                add_later(i)
+                times_gate(i)
+            store_dc(0)
             turned = turn_z(0)
             quantise_z(0, turned)
-            d2 = turn_down(2)
-            d3 = turn_down(3)
-            quantise_down(2, d2)
-            quantise_down(3, d3)
-
+            stage1(4)
+            add_later(4)
+            times_gate(4)
             for i in range(0, TT, 2):
-                banks = stage2(i)
-                if i + 2 < TT:
-                    stage1(i + 2)
-                finish(i, banks)
-                if i + 2 < TT:
-                    add_later(i + 2)
-                banks = stage2(i + 1)
-                if i + 2 < TT:
-                    stage1(i + 3)
-                    finish(i + 1, banks)
-                    add_later(i + 3)
-                    times_gate(i + 2)
-                    times_gate(i + 3)
-                    if (i + 4) % HALF == 0:
-                        store_dc((i + 2) // HALF)
-                    turned = turn_z(i + 2)
-                    quantise_z(i + 2, turned)
-                else:
-                    finish(i + 1, banks)
+                for j in range(i, i + 2):
+                    banks = stage2(j)
+                    if j + 5 < TT:
+                        stage1(j + 5)
+                    if j == i and i + 2 < TT:
+                        turned = turn_z(i + 2)
+                    finish(j, banks)
+                    if j + 5 < TT:
+                        add_later(j + 5)
+                        times_gate(j + 5)
+                    if j == i and i + 2 < TT:
+                        quantise_z(i + 2, turned)
+                if i == 2:
+                    store_dc(1)

@@ -139,6 +139,16 @@ def tile_latent_cache_backward_e3_kernel(
             pairs = []
             for j in range(PASSES // 2):
                 pairs.append(group.tile([P, 2, R, 4], BF16, name="grouped", tag="grouped", align_bytes=64))
+            def quantise_up(j, first, end):
+                cols = slice(first * P, end * P)
+                for gg in range(2):
+                    nc.vector.quantize_mx(
+                        out=up_codes[:, 2 * j + gg, cols].bitcast(E4M3),
+                        scales=up_scales[:, 2 * j + gg, cols],
+                        in_=pairs[j][:, gg, cols, :].rearrange("p r j -> p (r j)"),
+                    )
+
+            ready = []
             for rt in range(RT):
                 words = up_raw[rt][:].bitcast(F32)
                 for j in range(PASSES // 2):
@@ -154,17 +164,14 @@ def tile_latent_cache_backward_e3_kernel(
                     copy_out(
                         out=dst[:, :, rt * P : (rt + 1) * P, :], in_=bank[:].rearrange("p g u r -> p g r u")
                     )
-                    if rt == RT - 1:
-                        for gg in range(2):
-                            g = 2 * j + gg
-                            nc.vector.quantize_mx(
-                                out=up_codes[:, g, :].bitcast(E4M3),
-                                scales=up_scales[:, g, :],
-                                in_=pairs[j][:, gg, :, :].rearrange("p r j -> p (r j)"),
-                            )
+                    if rt > 0:
+                        ready.append((j, 0 if rt == 1 else rt, rt + 1))
+                    while len(ready) > 1 or (ready and rt == RT - 1 and j == PASSES // 2 - 1):
+                        quantise_up(*ready.pop(0))
 
             acc = {}
             z_tiles = {}
+            z_grouped = {}
             z_codes = {}
             dc_half = {}
 
@@ -209,31 +216,27 @@ def tile_latent_cache_backward_e3_kernel(
                     in_=dc_half[h][:],
                 )
 
-            def turn_z(i0):
-                bank = work.tile([P, 2, 2, P], F32, name="bank", tag="bank")
-                for i in range(2):
-                    words = z_tiles[i0 + i][:].bitcast(F32)
-                    for u in range(2):
-                        nc.tensor.transpose(bank[:, i, u, :], words[:, u : R // 2 : 2], ident[:])
-                grouped = small.tile([P, 2, P, 4], BF16, name="z_grouped", tag="z_grouped", bufs=2, align_bytes=64)
-                dst = grouped[:].rearrange("p i t j -> p (i t j)").bitcast(F32)
+            def turn_z(i):
+                words = z_tiles[i][:].bitcast(F32)
+                bank = work.tile([P, 2, P], F32, name="bank", tag="bank")
+                for u in range(2):
+                    nc.tensor.transpose(bank[:, u, :], words[:, u : R // 2 : 2], ident[:])
+                grouped = small.tile([P, P, 4], BF16, name="z_grouped", tag="z_grouped", align_bytes=64)
+                dst = grouped[:].rearrange("p t j -> p (t j)").bitcast(F32)
                 nc.scalar.copy(
-                    out=dst.rearrange("p (i t u) -> p i t u", i=2, u=2),
-                    in_=bank[:].rearrange("p i u t -> p i t u"),
+                    out=dst.rearrange("p (t u) -> p t u", u=2), in_=bank[:].rearrange("p u t -> p t u")
                 )
-                return grouped
+                z_grouped[i] = grouped
 
-            def quantise_z(i0, grouped):
-                codes = small.tile([P, 2 * P], U32, name="z_code", tag="z_code", align_bytes=64)
-                scales = small.tile([P, 2 * P], U8, name="z_scale", tag="z_scale", align_bytes=64)
+            def quantise_z(i):
+                codes = small.tile([P, P], U32, name="z_code", tag="z_code", align_bytes=64)
+                scales = small.tile([P, P], U8, name="z_scale", tag="z_scale", align_bytes=64)
                 nc.vector.quantize_mx(
                     out=codes[:].bitcast(E5M2),
                     scales=scales[:],
-                    in_=grouped[:].rearrange("p i t j -> p (i t j)"),
+                    in_=z_grouped[i][:].rearrange("p t j -> p (t j)"),
                 )
-                for i in range(2):
-                    cols = slice(i * P, (i + 1) * P)
-                    z_codes[i0 + i] = (codes[:, cols], scales[:, cols])
+                z_codes[i] = (codes[:], scales[:])
 
             def stage2(i):
                 codes, scales = z_codes[i]
@@ -260,36 +263,30 @@ def tile_latent_cache_backward_e3_kernel(
                     nc.vector.tensor_tensor(out=dh[:, cols], in0=banks[b][:], in1=skip[:, i, cols], op=ADD)
                 nc.sync.dma_start(out=out_dh[i * P : (i + 1) * P, :], in_=dh[:])
 
-            open_acc(0)
-            open_acc(1)
-            for g in range(PASSES):
-                for i in range(2):
-                    stage1_pass(i, g)
-            for i in range(2):
+            def dc_and_z(i):
                 add_later(i)
                 times_gate(i)
-            for i in range(2, 4):
-                stage1(i)
-                add_later(i)
-                times_gate(i)
-            store_dc(0)
-            turned = turn_z(0)
-            quantise_z(0, turned)
-            stage1(4)
-            add_later(4)
-            times_gate(4)
-            for i in range(0, TT, 2):
-                for j in range(i, i + 2):
-                    banks = stage2(j)
-                    if j + 5 < TT:
-                        stage1(j + 5)
-                    if j == i and i + 2 < TT:
-                        turned = turn_z(i + 2)
-                    finish(j, banks)
-                    if j + 5 < TT:
-                        add_later(j + 5)
-                        times_gate(j + 5)
-                    if j == i and i + 2 < TT:
-                        quantise_z(i + 2, turned)
-                if i == 2:
-                    store_dc(1)
+                if i % HALF == HALF - 1:
+                    store_dc(i // HALF)
+
+            stage1(0)
+            dc_and_z(0)
+            stage1(1)
+            dc_and_z(1)
+            turn_z(0)
+            quantise_z(0)
+            stage1(2)
+            dc_and_z(2)
+            turn_z(1)
+            quantise_z(1)
+            for i in range(TT):
+                banks = stage2(i)
+                if i + 3 < TT:
+                    stage1(i + 3)
+                if i + 2 < TT:
+                    turn_z(i + 2)
+                finish(i, banks)
+                if i + 3 < TT:
+                    dc_and_z(i + 3)
+                if i + 2 < TT:
+                    quantise_z(i + 2)

@@ -33,8 +33,8 @@ def tile_latent_cache_backward_e3_kernel(
         stage = ctx.enter_context(tc.tile_pool(name="stage", bufs=8))
         group = ctx.enter_context(tc.tile_pool(name="group", bufs=4))
         small = ctx.enter_context(tc.tile_pool(name="small", bufs=4))
-        accs = ctx.enter_context(tc.psum_pool(name="accs", bufs=4))
-        work = ctx.enter_context(tc.psum_pool(name="work", bufs=4))
+        accs = ctx.enter_context(tc.psum_pool(name="accs", bufs=2))
+        work = ctx.enter_context(tc.psum_pool(name="work", bufs=6))
 
         ident = keep.tile([P, P], F32, name="ident")
         make_identity(nc, ident[:])
@@ -56,14 +56,6 @@ def tile_latent_cache_backward_e3_kernel(
                     out=g_scales[32 * q : 32 * q + 4, :, :].bitcast(I32),
                     in_=dkv_scales[:, 4 * q : 4 * q + 4, :].rearrange("g q n -> q g n").bitcast(I32),
                 )
-            down_raw = []
-            for h in range(2):
-                raw = stage.tile([P, 2, 4, R], BF16, name="down_raw", tag="stage", align_bytes=64)
-                nc.sync.dma_start(
-                    out=raw[:].rearrange("p b a r -> p b (a r)"),
-                    in_=w_down[h * 1024 : (h + 1) * 1024, :].rearrange("(b p a) r -> p b (a r)", p=P, a=4),
-                )
-                down_raw.append(raw)
             up_raw = []
             for rt in range(RT):
                 raw = stage.tile([P, F], BF16, name="up_raw", tag="stage", align_bytes=64)
@@ -83,23 +75,37 @@ def tile_latent_cache_backward_e3_kernel(
                     in_=src[h * (T // 2) : (h + 1) * (T // 2), :].rearrange("(i p) r -> p i r", p=P),
                 )
 
+            down_raw = []
+
+            def load_down(h):
+                raw = stage.tile([P, 2, 4, R], BF16, name="down_raw", tag="stage", align_bytes=64)
+                nc.sync.dma_start(
+                    out=raw[:].rearrange("p b a r -> p b (a r)"),
+                    in_=w_down[h * 1024 : (h + 1) * 1024, :].rearrange("(b p a) r -> p b (a r)", p=P, a=4),
+                )
+                down_raw.append(raw)
+
+            load_down(0)
+            load_down(1)
             load_g(0, 0)
             load_g(4, 0)
             load_half(later, dc_later, 0)
             load_half(gates, gate, 0)
-            for i in range(TT):
-                if i == 1:
+            for i in range(0, TT, 2):
+                if i == 2:
                     load_g(0, 1)
                     load_g(4, 1)
                     load_half(later, dc_later, 1)
                     load_half(gates, gate, 1)
-                nc.sync.dma_start(out=skip[:, i, :], in_=dh_skip[i * P : (i + 1) * P, :])
+                nc.sync.dma_start(
+                    out=skip[:, i : i + 2, :], in_=dh_skip[i * P : (i + 2) * P, :].rearrange("(i p) d -> p i d", p=P)
+                )
 
             count = [0]
 
             def copy_out(out, in_):
                 count[0] += 1
-                if count[0] % 3 == 0:
+                if count[0] % 5 == 0:
                     nc.vector.tensor_copy(out=out, in_=in_)
                 else:
                     nc.scalar.copy(out=out, in_=in_)
@@ -130,12 +136,6 @@ def tile_latent_cache_backward_e3_kernel(
                     in_=grouped[:].rearrange("p d j -> p (d j)"),
                 )
 
-            turned = [turn_down(0), turn_down(1)]
-            quantise_down(0, turned[0])
-            quantise_down(1, turned[1])
-            turned = [turn_down(2), turn_down(3)]
-            quantise_down(2, turned[0])
-            quantise_down(3, turned[1])
             pairs = []
             for j in range(PASSES // 2):
                 pairs.append(group.tile([P, 2, R, 4], BF16, name="grouped", tag="grouped", align_bytes=64))
@@ -269,13 +269,25 @@ def tile_latent_cache_backward_e3_kernel(
                 if i % HALF == HALF - 1:
                     store_dc(i // HALF)
 
-            stage1(0)
+            d0 = turn_down(0)
+            d1 = turn_down(1)
+            quantise_down(0, d0)
+            quantise_down(1, d1)
+            d2 = turn_down(2)
+            d3 = turn_down(3)
+            quantise_down(2, d2)
+            quantise_down(3, d3)
+            for i in range(2):
+                open_acc(i)
+            for g0 in range(0, PASSES, 4):
+                for i in range(2):
+                    for g in range(g0, g0 + 4):
+                        stage1_pass(i, g)
             dc_and_z(0)
-            stage1(1)
             dc_and_z(1)
+            stage1(2)
             turn_z(0)
             quantise_z(0)
-            stage1(2)
             dc_and_z(2)
             turn_z(1)
             quantise_z(1)
@@ -283,9 +295,9 @@ def tile_latent_cache_backward_e3_kernel(
                 banks = stage2(i)
                 if i + 3 < TT:
                     stage1(i + 3)
+                finish(i, banks)
                 if i + 2 < TT:
                     turn_z(i + 2)
-                finish(i, banks)
                 if i + 3 < TT:
                     dc_and_z(i + 3)
                 if i + 2 < TT:

@@ -51,11 +51,6 @@ def tile_latent_cache_backward_e3_kernel(
 
         with tc.manual_schedule():
             nc.vector.memset(g_scales[:].rearrange("p g n -> p (g n)").bitcast(I32), 0)
-            for q in range(4):
-                nc.gpsimd.dma_start(
-                    out=g_scales[32 * q : 32 * q + 4, :, :].bitcast(I32),
-                    in_=dkv_scales[:, 4 * q : 4 * q + 4, :].rearrange("g q n -> q g n").bitcast(I32),
-                )
             up_raw = []
             for rt in range(RT):
                 raw = stage.tile([P, F], BF16, name="up_raw", tag="stage", align_bytes=64)
@@ -86,6 +81,11 @@ def tile_latent_cache_backward_e3_kernel(
                 down_raw.append(raw)
 
             load_down(0)
+            for r in range(4):
+                nc.sync.dma_start(
+                    out=g_scales[r:P:32, :, :].bitcast(I32),
+                    in_=dkv_scales[:, r:16:4, :].rearrange("g q n -> q g n").bitcast(I32),
+                )
             load_down(1)
             load_g(0, 0)
             load_g(4, 0)

from contextlib import ExitStack

import concourse.mybir as mybir
from concourse.masks import make_identity

T, F, R, D = 1024, 4096, 512, 2048
FLOPS = 2 * T * F * R + 2 * T * R * D

F32 = mybir.dt.float32
BF16 = mybir.dt.bfloat16
U32 = mybir.dt.uint32
I32 = mybir.dt.int32
U8 = mybir.dt.uint8
E4M3 = mybir.dt.float8_e4m3fn_x4
E5M2 = mybir.dt.float8_e5m2_x4
ADD = mybir.AluOpType.add
MULT = mybir.AluOpType.mult

P = 128
PASSES = F // 512
RT = R // P
TT = T // P
HALF = TT // 2
DB = D // 512


def tile_latent_cache_backward_e3_kernel(
    tc, dkv_words, dkv_scales, w_up, dc_later, gate, w_down, dh_skip, out_dc, out_dh
):
    nc = tc.nc
    with ExitStack() as ctx:
        keep = ctx.enter_context(tc.tile_pool(name="keep", bufs=1))
        stage = ctx.enter_context(tc.tile_pool(name="stage", bufs=8))
        group = ctx.enter_context(tc.tile_pool(name="group", bufs=4))
        small = ctx.enter_context(tc.tile_pool(name="small", bufs=4))
        accs = ctx.enter_context(tc.psum_pool(name="accs", bufs=2))
        work = ctx.enter_context(tc.psum_pool(name="work", bufs=6))

        ident = keep.tile([P, P], F32, name="ident")
        make_identity(nc, ident[:])

        g_words = keep.tile([P, PASSES, T], U32, name="g_words", align_bytes=64)
        g_scales = keep.tile([P, PASSES, T], U8, name="g_scales", align_bytes=64)
        up_codes = keep.tile([P, PASSES, R], U32, name="up_codes", align_bytes=64)
        up_scales = keep.tile([P, PASSES, R], U8, name="up_scales", align_bytes=64)
        down_codes = keep.tile([P, D], U32, name="down_codes", align_bytes=64)
        down_scales = keep.tile([P, D], U8, name="down_scales", align_bytes=64)
        skip = keep.tile([P, TT, D], BF16, name="skip", align_bytes=64)
        later = keep.tile([P, TT, R], BF16, name="later", align_bytes=64)
        gates = keep.tile([P, TT, R], BF16, name="gates", align_bytes=64)

        with tc.manual_schedule():
            nc.vector.memset(g_scales[:].rearrange("p g n -> p (g n)").bitcast(I32), 0)
            up_raw = []
            for rt in range(RT):
                raw = stage.tile([P, F], BF16, name="up_raw", tag="stage", align_bytes=64)
                nc.sync.dma_start(out=raw[:], in_=w_up[rt * P : (rt + 1) * P, :])
                up_raw.append(raw)

            def load_g(g, h):
                cols = slice(h * (T // 2), (h + 1) * (T // 2))
                nc.sync.dma_start(
                    out=g_words[:, g : g + 4, cols].bitcast(I32),
                    in_=dkv_words[g : g + 4, :, cols, :].rearrange("g p n t -> p g (n t)").bitcast(I32),
                )

            def load_half(tile, src, h):
                nc.sync.dma_start(
                    out=tile[:, h * HALF : (h + 1) * HALF, :],
                    in_=src[h * (T // 2) : (h + 1) * (T // 2), :].rearrange("(i p) r -> p i r", p=P),
                )

            down_raw = []

            def load_down(h):
                raw = stage.tile([P, 2, 4, R], BF16, name="down_raw", tag="stage", align_bytes=64)
                nc.sync.dma_start(
                    out=raw[:].rearrange("p b a r -> p b (a r)"),
                    in_=w_down[h * 1024 : (h + 1) * 1024, :].rearrange("(b p a) r -> p b (a r)", p=P, a=4),
                )
                down_raw.append(raw)

            load_down(0)
            for r in range(4):
                nc.sync.dma_start(
                    out=g_scales[r:P:32, :, :].bitcast(I32),
                    in_=dkv_scales[:, r:16:4, :].rearrange("g q n -> q g n").bitcast(I32),
                )
            load_down(1)
            load_g(0, 0)
            load_g(4, 0)
            load_half(later, dc_later, 0)
            load_half(gates, gate, 0)
            for i in range(0, TT, 2):
                if i == 2:
                    load_g(0, 1)
                    load_g(4, 1)
                    load_half(later, dc_later, 1)
                    load_half(gates, gate, 1)
                nc.sync.dma_start(
                    out=skip[:, i : i + 2, :], in_=dh_skip[i * P : (i + 2) * P, :].rearrange("(i p) d -> p i d", p=P)
                )

            count = [0]

            def copy_out(out, in_):
                count[0] += 1
                if count[0] % 5 == 0:
                    nc.vector.tensor_copy(out=out, in_=in_)
                else:
                    nc.scalar.copy(out=out, in_=in_)

            def turn_down(b):
                words = down_raw[b // 2][:].rearrange("p b a r -> p (b a r)").bitcast(F32)
                grouped = group.tile([P, 512, 4], BF16, name="grouped", tag="grouped", align_bytes=64)
                dst = grouped[:].rearrange("p d j -> p (d j)").bitcast(F32)
                dst = dst.rearrange("p (q a u) -> p q a u", a=4, u=2)
                for half in range(2):
                    bank = work.tile([P, 2, 2, P], F32, name="bank", tag="bank")
                    for aa in range(2):
                        first = (b % 2) * 1024 + (2 * half + aa) * 256
                        for u in range(2):
                            nc.tensor.transpose(
                                bank[:, aa, u, :], words[:, first + u : first + 256 : 2], ident[:]
                            )
                    copy_out(
                        out=dst[:, :, 2 * half : 2 * half + 2, :], in_=bank[:].rearrange("p a u q -> p q a u")
                    )
                return grouped

            def quantise_down(b, grouped):
                cols = slice(b * 512, (b + 1) * 512)
                nc.vector.quantize_mx(
                    out=down_codes[:, cols].bitcast(E4M3),
                    scales=down_scales[:, cols],
                    in_=grouped[:].rearrange("p d j -> p (d j)"),
                )

            pairs = []
            for j in range(PASSES // 2):
                pairs.append(group.tile([P, 2, R, 4], BF16, name="grouped", tag="grouped", align_bytes=64))
            def quantise_up(j, first, end):
                cols = slice(first * P, end * P)
                for gg in range(2):
                    nc.vector.quantize_mx(
                        out=up_codes[:, 2 * j + gg, cols].bitcast(E4M3),
                        scales=up_scales[:, 2 * j + gg, cols],
                        in_=pairs[j][:, gg, cols, :].rearrange("p r j -> p (r j)"),
                    )

            ready = []
            for rt in range(RT):
                words = up_raw[rt][:].bitcast(F32)
                for j in range(PASSES // 2):
                    bank = work.tile([P, 2, 2, P], F32, name="bank", tag="bank")
                    for gg in range(2):
                        for u in range(2):
                            first = 256 * (2 * j + gg)
                            nc.tensor.transpose(
                                bank[:, gg, u, :], words[:, first + u : first + 256 : 2], ident[:]
                            )
                    dst = pairs[j][:].rearrange("p g r j -> p (g r j)").bitcast(F32)
                    dst = dst.rearrange("p (g r u) -> p g r u", g=2, u=2)
                    copy_out(
                        out=dst[:, :, rt * P : (rt + 1) * P, :], in_=bank[:].rearrange("p g u r -> p g r u")
                    )
                    if rt > 0:
                        ready.append((j, 0 if rt == 1 else rt, rt + 1))
                    while len(ready) > 1 or (ready and rt == RT - 1 and j == PASSES // 2 - 1):
                        quantise_up(*ready.pop(0))

            acc = {}
            z_tiles = {}
            z_grouped = {}
            z_codes = {}
            dc_half = {}

            def stage1_pass(i, g):
                cols = slice(i * P, (i + 1) * P)
                nc.tensor.matmul_mx(
                    out=acc[i][:],
                    lhsT=g_words[:, g, cols].bitcast(E5M2),
                    lhsT_scale=g_scales[:, g, cols],
                    rhs=up_codes[:, g, :].bitcast(E4M3),
                    rhs_scale=up_scales[:, g, :],
                    start=(g == 0),
                    stop=(g == PASSES - 1),
                )

            def open_acc(i):
                acc[i] = accs.tile([P, R], F32, name="acc", tag="acc")

            def stage1(i):
                open_acc(i)
                for g in range(PASSES):
                    stage1_pass(i, g)

            def add_later(i):
                h = i // HALF
                if i % HALF == 0:
                    dc_half[h] = stage.tile([P, HALF, R], F32, name="dc_half", tag="stage", align_bytes=64)
                nc.vector.tensor_tensor(
                    out=dc_half[h][:, i % HALF, :], in0=acc[i][:], in1=later[:, i, :], op=ADD
                )

            def times_gate(i):
                z = small.tile([P, R], BF16, name="z", tag="z", align_bytes=64)
                nc.gpsimd.tensor_tensor(
                    out=z[:], in0=dc_half[i // HALF][:, i % HALF, :], in1=gates[:, i, :], op=MULT
                )
                z_tiles[i] = z

            def store_dc(h):
                nc.sync.dma_start(
                    out=out_dc[h * (T // 2) : (h + 1) * (T // 2), :].rearrange("(i p) r -> p i r", p=P),
                    in_=dc_half[h][:],
                )

            def turn_z(i):
                words = z_tiles[i][:].bitcast(F32)
                bank = work.tile([P, 2, P], F32, name="bank", tag="bank")
                for u in range(2):
                    nc.tensor.transpose(bank[:, u, :], words[:, u : R // 2 : 2], ident[:])
                grouped = small.tile([P, P, 4], BF16, name="z_grouped", tag="z_grouped", align_bytes=64)
                dst = grouped[:].rearrange("p t j -> p (t j)").bitcast(F32)
                nc.scalar.copy(
                    out=dst.rearrange("p (t u) -> p t u", u=2), in_=bank[:].rearrange("p u t -> p t u")
                )
                z_grouped[i] = grouped

            def quantise_z(i):
                codes = small.tile([P, P], U32, name="z_code", tag="z_code", align_bytes=64)
                scales = small.tile([P, P], U8, name="z_scale", tag="z_scale", align_bytes=64)
                nc.vector.quantize_mx(
                    out=codes[:].bitcast(E5M2),
                    scales=scales[:],
                    in_=z_grouped[i][:].rearrange("p t j -> p (t j)"),
                )
                z_codes[i] = (codes[:], scales[:])

            def stage2(i):
                codes, scales = z_codes[i]
                banks = []
                for b in range(DB):
                    cols = slice(b * 512, (b + 1) * 512)
                    bank = work.tile([P, 512], F32, name="bank", tag="bank")
                    nc.tensor.matmul_mx(
                        out=bank[:],
                        lhsT=codes.bitcast(E5M2),
                        lhsT_scale=scales,
                        rhs=down_codes[:, cols].bitcast(E4M3),
                        rhs_scale=down_scales[:, cols],
                        start=True,
                        stop=True,
                    )
                    banks.append(bank)
                return banks

            def finish(i, banks):
                dh = stage.tile([P, D], F32, name="dh", tag="stage", align_bytes=64)
                for b in range(DB):
                    cols = slice(b * 512, (b + 1) * 512)
                    nc.vector.tensor_tensor(out=dh[:, cols], in0=banks[b][:], in1=skip[:, i, cols], op=ADD)
                nc.sync.dma_start(out=out_dh[i * P : (i + 1) * P, :], in_=dh[:])

            def dc_and_z(i):
                add_later(i)
                times_gate(i)
                if i % HALF == HALF - 1:
                    store_dc(i // HALF)

            d0 = turn_down(0)
            d1 = turn_down(1)
            quantise_down(0, d0)
            quantise_down(1, d1)
            d2 = turn_down(2)
            d3 = turn_down(3)
            quantise_down(2, d2)
            quantise_down(3, d3)
            for i in range(2):
                open_acc(i)
            for g0 in range(0, PASSES, 4):
                for i in range(2):
                    for g in range(g0, g0 + 4):
                        stage1_pass(i, g)
            dc_and_z(0)
            dc_and_z(1)
            stage1(2)
            turn_z(0)
            quantise_z(0)
            dc_and_z(2)
            turn_z(1)
            quantise_z(1)
            for i in range(TT):
                banks = stage2(i)
                if i + 3 < TT:
                    stage1(i + 3)
                finish(i, banks)
                if i + 2 < TT:
                    turn_z(i + 2)
                if i + 3 < TT:
                    dc_and_z(i + 3)
                if i + 2 < TT:
                    quantise_z(i + 2)
